import numpy as np
import ml_dtypes


def mxq(x, axis, fmt="e4m3"):
    dtype, down = {"e4m3": (ml_dtypes.float8_e4m3fn, 7), "e5m2": (ml_dtypes.float8_e5m2, 14)}[fmt]
    v = np.moveaxis(np.asarray(x, np.float32).astype(ml_dtypes.bfloat16).astype(np.float64), axis, -1)
    blocks = v.reshape(v.shape[:-1] + (-1, 32))
    amax = np.abs(blocks).max(-1, keepdims=True)
    byte = np.maximum(np.where(amax > 0, np.frexp(amax)[1] - 1 + 127, 0) - down, 1)
    scale = np.exp2(byte - 127.0)
    codes = (blocks / scale).astype(np.float32).astype(dtype).astype(np.float64)
    return np.moveaxis((codes * scale).reshape(v.shape), -1, axis)


WIDE = False


def mx_kscale(k):
    if not WIDE:
        return np.ones(k)
    levels = np.array([10, -10, 5, -5, 0])
    if k % 512:
        return np.exp2(np.random.permutation(np.resize(levels, k // 32))).repeat(32)
    a = np.empty((k // 512, 16))
    for p in range(k // 512):
        a[p, :8] = np.random.permutation(np.resize(levels, 8))
        for g in range(8):
            far = levels[np.abs(levels - a[p, g]) >= 10]
            a[p, g + 8] = far[np.random.randint(len(far))]
    return np.exp2(a.ravel()).repeat(32)


def f64(x):
    return np.asarray(x).astype(np.float64)


def striped8(idx):
    return np.asarray(idx).reshape(8, -1, 16).transpose(0, 2, 1).reshape(128, -1).astype(np.uint16)


def unstriped8(offs):
    return offs.reshape(8, 16, -1).transpose(0, 2, 1).reshape(8, -1).astype(np.int64)


def pick8(x, idx, run):
    r = np.arange(len(x))
    return x[r[:, None], idx[r % (8 * run) // run]]


E2M1 = np.array([0.0, 0.5, 1.0, 1.5, 2.0, 3.0, 4.0, 6.0, -0.0, -0.5, -1.0, -1.5, -2.0, -3.0, -4.0, -6.0])


def pack_weight(w, fmt):
    k, n = w.shape
    w = f64(np.asarray(w, np.float32).astype(ml_dtypes.bfloat16)).reshape(k // 32, 32, n)
    amax = np.abs(w).max(1)
    if fmt == "e4m3":
        byte = np.frexp(amax)[1] - 1 + 127 - 7
    else:
        mant, ex = np.frexp(amax / 6.0)
        byte = np.where(mant > 0.5, ex, ex - 1) + 127
    byte = np.clip(np.where(amax > 0, byte, 1), 1, 254)
    scaled = (w * np.exp2(127.0 - byte)[:, None, :]).reshape(k, n).astype(np.float32)
    by_word = np.ascontiguousarray(scaled.reshape(k // 512, 128, 4, n).transpose(0, 1, 3, 2))
    if fmt == "e4m3":
        words = by_word.astype(ml_dtypes.float8_e4m3fn).view(np.uint8)
    else:
        c = by_word.astype(ml_dtypes.float4_e2m1fn).view(np.uint8) & 0xF
        words = (c[..., 0::2] | (c[..., 1::2] << 4)).reshape(k // 512, 128, 2 * n)
    return np.ascontiguousarray(words), np.ascontiguousarray(byte.astype(np.uint8).reshape(k // 512, 16, n))


def unpack_weight(words, scales, fmt):
    g, _, n = scales.shape
    words = np.ascontiguousarray(words).reshape(g, 128, n, -1)
    if fmt == "e4m3":
        vals = words.view(ml_dtypes.float8_e4m3fn).astype(np.float64)
    else:
        nib = np.empty((g, 128, n, 4), np.uint8)
        nib[..., 0::2] = words & 0xF
        nib[..., 1::2] = words >> 4
        vals = E2M1[nib]
    vals = vals * np.repeat(np.exp2(scales.astype(np.float64) - 127.0), 8, axis=1)[..., None]
    return vals.transpose(0, 1, 3, 2).reshape(g * 512, n)


D, T, U, I, Q = 512, 1024, 1024, 512, 128


def setup_inputs():
    n = np.random.standard_normal
    idx = np.stack([np.random.permutation(T)[:I] for _ in range(8)])
    idx2 = np.stack([np.random.permutation(U)[:I] for _ in range(8)])
    idx3 = np.stack([np.random.permutation(U)[:I] for _ in range(8)])
    idx4 = np.stack([np.random.permutation(T)[:I] for _ in range(8)])
    idx5 = np.stack([np.random.permutation(T)[:I] for _ in range(8)])
    fd = mx_kscale(D)
    keysp = pack_weight(n((D, T)) / fd[:, None], "e4m3")
    notesp = pack_weight(n((D, U)) / fd[:, None], "e2m1")
    return {
        "query": (n((D, Q)) * 1.0 / np.sqrt(D) * fd[:, None]).astype(np.float32),
        "keys_words": keysp[0],
        "keys_scales": keysp[1],
        "notes_words": notesp[0],
        "notes_scales": notesp[1],
        "offs": striped8(idx),
        "offs2": striped8(idx2),
        "offs3": striped8(idx3),
        "offs4": striped8(idx4),
        "offs5": striped8(idx5),
    }


def reference(query, keys_words, keys_scales, notes_words, notes_scales, offs, offs2, offs3, offs4, offs5):
    idx = unstriped8(offs)
    idx2 = unstriped8(offs2)
    idx3 = unstriped8(offs3)
    idx4 = unstriped8(offs4)
    idx5 = unstriped8(offs5)
    keysu = unpack_weight(keys_words, keys_scales, "e4m3")
    notesu = unpack_weight(notes_words, notes_scales, "e2m1")
    queryq = mxq(f64(query), 0, "e4m3")
    a = queryq.T @ keysu
    b = queryq.T @ notesu
    f1 = np.zeros((Q, U))
    f1[np.arange(Q)[:, None], idx2[np.arange(Q) % 128 // 16]] = pick8(a, idx, 16)
    bb = f1 - b
    v = np.maximum(pick8(bb, idx3, 16), pick8(a, idx, 16))
    f2 = np.zeros((Q, T))
    f2[np.arange(Q)[:, None], idx4[np.arange(Q) % 128 // 16]] = v
    aa = a - f2
    y = pick8(aa, idx5, 16)
    return y

@@ -1,0 +1,157 @@
+from contextlib import ExitStack
+
+import concourse.mybir as mybir
+
+D, T, U, SLOTS, Q = 512, 1024, 1024, 512, 128
+FLOPS = 2 * D * Q * (T + U)
+
+F32 = mybir.dt.float32
+BF16 = mybir.dt.bfloat16
+I32 = mybir.dt.int32
+U32 = mybir.dt.uint32
+U16 = mybir.dt.uint16
+U8 = mybir.dt.uint8
+FP8X4 = mybir.dt.float8_e4m3fn_x4
+FP4X4 = mybir.dt.float4_e2m1fn_x4
+ALU = mybir.AluOpType
+COPY = mybir.ActivationFunctionType.Copy
+
+P = 128
+PACK = 4
+PER_COL = 16
+HALF = SLOTS // 2
+A_PIECE = 256
+B_PIECE = 512
+V_COLS = 704
+
+
+def load_scale_rows(nc, plane, scales):
+    for quad in range(4):
+        nc.sync.dma_start(
+            out=plane[32 * quad : 32 * quad + 4, :].bitcast(I32),
+            in_=scales[0, 4 * quad : 4 * quad + 4, :].bitcast(I32),
+        )
+
+
+def half_of(offsets, h):
+    cols = HALF // PER_COL
+    return offsets[:, h * cols : (h + 1) * cols]
+
+
+def gather_halves(nc, dst, window, offsets):
+    nc.vector.tensor_copy(dst[:, 0:HALF], window[:].indirect(half_of(offsets, 0)))
+    nc.scalar.activation(dst[:, HALF:SLOTS], window[:].indirect(half_of(offsets, 1)), COPY)
+
+
+def tile_attend_returnticket_two_kernel(
+    tc, query, keys_words, keys_scales, notes_words, notes_scales, offs, offs2, offs3, offs4, offs5, out
+):
+    nc = tc.nc
+    with ExitStack() as ctx:
+        sb = ctx.enter_context(tc.tile_pool(name="sb", bufs=1))
+        ps = ctx.enter_context(tc.psum_pool(name="ps", bufs=1))
+
+        idx = sb.tile([P, SLOTS // PER_COL], U16, name="idx")
+        idx2 = sb.tile([P, SLOTS // PER_COL], U16, name="idx2")
+        idx3 = sb.tile([P, SLOTS // PER_COL], U16, name="idx3")
+        idx4 = sb.tile([P, SLOTS // PER_COL], U16, name="idx4")
+        idx5 = sb.tile([P, SLOTS // PER_COL], U16, name="idx5")
+
+        q_raw = sb.tile([P, PACK, Q], F32, name="q_raw")
+        q_bf = sb.tile([P, Q, PACK], BF16, name="q_bf", align_bytes=64)
+        q_codes = sb.tile([P, Q], U32, name="q_codes", align_bytes=64)
+        q_plane = sb.tile([P, Q], U8, name="q_plane", align_bytes=64)
+        k_codes = sb.tile([P, T], U32, name="k_codes", align_bytes=64)
+        k_plane = sb.tile([P, T], U8, name="k_plane", align_bytes=64)
+        n_codes = sb.tile([P, 2 * U], U8, name="n_codes", align_bytes=64)
+        n_plane = sb.tile([P, U], U8, name="n_plane", align_bytes=64)
+
+        a = sb.tile([P, T], F32, name="a")
+        f1 = sb.tile([P, U], F32, name="f1")
+        bb = sb.tile([P, U], F32, name="bb")
+        f2 = sb.tile([P, T], F32, name="f2")
+        aa = sb.tile([P, T], F32, name="aa")
+        own = sb.tile([P, SLOTS], F32, name="own")
+        back = sb.tile([P, SLOTS], F32, name="back")
+        v = sb.tile([P, SLOTS], F32, name="v")
+        res = sb.tile([P, SLOTS], F32, name="res")
+
+        nc.vector.memset(k_plane[:].bitcast(U32), 0)
+        nc.vector.memset(n_plane[:].bitcast(U32), 0)
+        nc.vector.memset(f1[:], 0.0)
+        nc.vector.memset(f2[:], 0.0)
+
+        nc.sync.dma_start(out=q_raw[:], in_=query.rearrange("(p j) q -> p j q", j=PACK))
+        nc.sync.dma_start(
+            out=k_codes[:].bitcast(I32), in_=keys_words[0].rearrange("p n t -> p (n t)").bitcast(I32)
+        )
+        load_scale_rows(nc, k_plane, keys_scales)
+        nc.sync.dma_start(idx[:], offs)
+        nc.sync.dma_start(idx2[:], offs2)
+        nc.sync.dma_start(idx3[:], offs3)
+        nc.sync.dma_start(out=n_codes[:].bitcast(I32), in_=notes_words[0].bitcast(I32))
+        load_scale_rows(nc, n_plane, notes_scales)
+        nc.sync.dma_start(idx4[:], offs4)
+        nc.sync.dma_start(idx5[:], offs5)
+
+        nc.vector.tensor_copy(
+            out=q_bf[:].rearrange("p (c i) t -> p c t i", i=4),
+            in_=q_raw[:].rearrange("p t (c i) -> p c t i", i=4),
+        )
+        nc.vector.quantize_mx(
+            out=q_codes[:].bitcast(FP8X4), scales=q_plane[:], in_=q_bf[:].rearrange("p q t -> p (q t)")
+        )
+
+        a_banks = []
+        for piece in range(T // A_PIECE):
+            cols = slice(piece * A_PIECE, (piece + 1) * A_PIECE)
+            bank = ps.tile([P, A_PIECE], F32, name="a_bank%d" % piece)
+            nc.tensor.matmul_mx(
+                out=bank[:],
+                lhsT=q_codes[:].bitcast(FP8X4),
+                lhsT_scale=q_plane[:],
+                rhs=k_codes[:, cols].bitcast(FP8X4),
+                rhs_scale=k_plane[:, cols],
+                start=True,
+                stop=True,
+            )
+            if piece % 2 == 0:
+                nc.scalar.activation(a[:, cols], bank[:], COPY)
+            else:
+                nc.vector.tensor_copy(a[:, cols], bank[:])
+            a_banks.append(bank)
+
+        b_banks = []
+        for piece in range(U // B_PIECE):
+            bank = ps.tile([P, B_PIECE], F32, name="b_bank%d" % piece)
+            nc.tensor.matmul_mx(
+                out=bank[:],
+                lhsT=q_codes[:].bitcast(FP8X4),
+                lhsT_scale=q_plane[:],
+                rhs=n_codes[:, 2 * piece * B_PIECE : 2 * (piece + 1) * B_PIECE].bitcast(FP4X4),
+                rhs_scale=n_plane[:, piece * B_PIECE : (piece + 1) * B_PIECE],
+                start=True,
+                stop=True,
+            )
+            b_banks.append(bank)
+
+        gather_halves(nc, own, a, idx)
+        b_tail = sb.tile([P, U - V_COLS], F32, name="b_tail")
+        nc.scalar.activation(b_tail[:], b_banks[1][:, V_COLS - B_PIECE : B_PIECE], COPY)
+        nc.vector.tensor_copy(f1[:].indirect(idx2[:]), own[:])
+        nc.gpsimd.tensor_tensor(bb[:, V_COLS:U], f1[:, V_COLS:U], b_tail[:], ALU.subtract)
+        for lo in range(0, V_COLS, B_PIECE):
+            hi = min(lo + B_PIECE, V_COLS)
+            nc.vector.tensor_tensor(bb[:, lo:hi], f1[:, lo:hi], b_banks[lo // B_PIECE][:, 0 : hi - lo], ALU.subtract)
+
+        gather_halves(nc, back, bb, idx3)
+        nc.vector.tensor_tensor(v[:], back[:], own[:], ALU.max)
+        nc.vector.tensor_copy(f2[:].indirect(idx4[:]), v[:])
+        nc.gpsimd.tensor_tensor(aa[:, V_COLS:T], a[:, V_COLS:T], f2[:, V_COLS:T], ALU.subtract)
+        for lo in range(0, V_COLS, A_PIECE):
+            hi = min(lo + A_PIECE, V_COLS)
+            nc.vector.tensor_tensor(aa[:, lo:hi], a_banks[lo // A_PIECE][:, 0 : hi - lo], f2[:, lo:hi], ALU.subtract)
+
+        gather_halves(nc, res, aa, idx5)
+        nc.sync.dma_start(out=out[:, 0:HALF], in_=res[:, 0:HALF])
+        nc.scalar.dma_start(out=out[:, HALF:SLOTS], in_=res[:, HALF:SLOTS])

@@ -20,9 +20,10 @@ P = 128
 PACK = 4
 PER_COL = 16
 HALF = SLOTS // 2
-A_PIECE = 256
+A_PIECES = (256, 256, 256, 128, 128)
 B_PIECE = 512
 V_COLS = 704
+V_QUERIES = 88
 
 
 def load_scale_rows(nc, plane, scales):
@@ -61,7 +62,7 @@ def tile_attend_returnticket_two_kernel(
         q_bf = sb.tile([P, Q, PACK], BF16, name="q_bf", align_bytes=64)
         q_codes = sb.tile([P, Q], U32, name="q_codes", align_bytes=64)
         q_plane = sb.tile([P, Q], U8, name="q_plane", align_bytes=64)
-        k_codes = sb.tile([P, T], U32, name="k_codes", align_bytes=64)
+        k_codes = [sb.tile([P, T // 2], U32, name="k_codes%d" % h, align_bytes=64) for h in range(2)]
         k_plane = sb.tile([P, T], U8, name="k_plane", align_bytes=64)
         n_codes = sb.tile([P, 2 * U], U8, name="n_codes", align_bytes=64)
         n_plane = sb.tile([P, U], U8, name="n_plane", align_bytes=64)
@@ -82,11 +83,11 @@ def tile_attend_returnticket_two_kernel(
         nc.vector.memset(f2[:], 0.0)
 
         nc.sync.dma_start(out=q_raw[:], in_=query.rearrange("(p j) q -> p j q", j=PACK))
-        nc.sync.dma_start(
-            out=k_codes[:].bitcast(I32), in_=keys_words[0].rearrange("p n t -> p (n t)").bitcast(I32)
-        )
-        load_scale_rows(nc, k_plane, keys_scales)
+        k_words = keys_words[0].rearrange("p n t -> p (n t)").bitcast(I32)
+        nc.sync.dma_start(out=k_codes[0][:].bitcast(I32), in_=k_words[:, 0 : T // 2])
         nc.sync.dma_start(idx[:], offs)
+        load_scale_rows(nc, k_plane, keys_scales)
+        nc.sync.dma_start(out=k_codes[1][:].bitcast(I32), in_=k_words[:, T // 2 : T])
         nc.sync.dma_start(idx2[:], offs2)
         nc.sync.dma_start(idx3[:], offs3)
         nc.sync.dma_start(out=n_codes[:].bitcast(I32), in_=notes_words[0].bitcast(I32))
@@ -95,22 +96,29 @@ def tile_attend_returnticket_two_kernel(
         nc.sync.dma_start(idx5[:], offs5)
 
         nc.vector.tensor_copy(
-            out=q_bf[:].rearrange("p (c i) t -> p c t i", i=4),
-            in_=q_raw[:].rearrange("p t (c i) -> p c t i", i=4),
+            out=q_bf[:, 0:V_QUERIES, :].rearrange("p (c i) t -> p c t i", i=4),
+            in_=q_raw[:, :, 0:V_QUERIES].rearrange("p t (c i) -> p c t i", i=4),
+        )
+        nc.scalar.activation(
+            q_bf[:, V_QUERIES:Q, :].rearrange("p (c i) t -> p c t i", i=4),
+            q_raw[:, :, V_QUERIES:Q].rearrange("p t (c i) -> p c t i", i=4),
+            COPY,
         )
         nc.vector.quantize_mx(
             out=q_codes[:].bitcast(FP8X4), scales=q_plane[:], in_=q_bf[:].rearrange("p q t -> p (q t)")
         )
 
         a_banks = []
-        for piece in range(T // A_PIECE):
-            cols = slice(piece * A_PIECE, (piece + 1) * A_PIECE)
-            bank = ps.tile([P, A_PIECE], F32, name="a_bank%d" % piece)
+        lo = 0
+        for piece, width in enumerate(A_PIECES):
+            cols = slice(lo, lo + width)
+            k_half, k_lo = divmod(lo, T // 2)
+            bank = ps.tile([P, width], F32, name="a_bank%d" % piece)
             nc.tensor.matmul_mx(
                 out=bank[:],
                 lhsT=q_codes[:].bitcast(FP8X4),
                 lhsT_scale=q_plane[:],
-                rhs=k_codes[:, cols].bitcast(FP8X4),
+                rhs=k_codes[k_half][:, k_lo : k_lo + width].bitcast(FP8X4),
                 rhs_scale=k_plane[:, cols],
                 start=True,
                 stop=True,
@@ -119,7 +127,8 @@ def tile_attend_returnticket_two_kernel(
                 nc.scalar.activation(a[:, cols], bank[:], COPY)
             else:
                 nc.vector.tensor_copy(a[:, cols], bank[:])
-            a_banks.append(bank)
+            a_banks.append((lo, width, bank))
+            lo = lo + width
 
         b_banks = []
         for piece in range(U // B_PIECE):
@@ -145,12 +154,15 @@ def tile_attend_returnticket_two_kernel(
             nc.vector.tensor_tensor(bb[:, lo:hi], f1[:, lo:hi], b_banks[lo // B_PIECE][:, 0 : hi - lo], ALU.subtract)
 
         gather_halves(nc, back, bb, idx3)
-        nc.vector.tensor_tensor(v[:], back[:], own[:], ALU.max)
+        for h in range(2):
+            cols = slice(h * HALF, (h + 1) * HALF)
+            nc.vector.tensor_tensor(v[:, cols], back[:, cols], own[:, cols], ALU.max)
         nc.vector.tensor_copy(f2[:].indirect(idx4[:]), v[:])
         nc.gpsimd.tensor_tensor(aa[:, V_COLS:T], a[:, V_COLS:T], f2[:, V_COLS:T], ALU.subtract)
-        for lo in range(0, V_COLS, A_PIECE):
-            hi = min(lo + A_PIECE, V_COLS)
-            nc.vector.tensor_tensor(aa[:, lo:hi], a_banks[lo // A_PIECE][:, 0 : hi - lo], f2[:, lo:hi], ALU.subtract)
+        for lo, width, bank in a_banks:
+            hi = min(lo + width, V_COLS)
+            if hi > lo:
+                nc.vector.tensor_tensor(aa[:, lo:hi], bank[:, 0 : hi - lo], f2[:, lo:hi], ALU.subtract)
 
         gather_halves(nc, res, aa, idx5)
         nc.sync.dma_start(out=out[:, 0:HALF], in_=res[:, 0:HALF])

@@ -23,6 +23,7 @@ HALF = SLOTS // 2
 A_PIECES = (256, 256, 256, 128, 128)
 B_PIECE = 512
 V_COLS = 704
+PLANE_COLS = T // 4
 V_QUERIES = 88
 
 
@@ -63,7 +64,7 @@ def tile_attend_returnticket_two_kernel(
         q_codes = sb.tile([P, Q], U32, name="q_codes", align_bytes=64)
         q_plane = sb.tile([P, Q], U8, name="q_plane", align_bytes=64)
         k_codes = [sb.tile([P, T // 2], U32, name="k_codes%d" % h, align_bytes=64) for h in range(2)]
-        k_plane = sb.tile([P, T], U8, name="k_plane", align_bytes=64)
+        k_plane = sb.tile([P, PLANE_COLS], U8, name="k_plane", align_bytes=64)
         n_codes = sb.tile([P, 2 * U], U8, name="n_codes", align_bytes=64)
         n_plane = sb.tile([P, U], U8, name="n_plane", align_bytes=64)
 
@@ -86,7 +87,11 @@ def tile_attend_returnticket_two_kernel(
         k_words = keys_words[0].rearrange("p n t -> p (n t)").bitcast(I32)
         nc.sync.dma_start(out=k_codes[0][:].bitcast(I32), in_=k_words[:, 0 : T // 2])
         nc.sync.dma_start(idx[:], offs)
-        load_scale_rows(nc, k_plane, keys_scales)
+        for quad in range(4):
+            nc.sync.dma_start(
+                out=k_plane[32 * quad : 32 * quad + 16, :].bitcast(I32),
+                in_=keys_scales[0, 4 * quad : 4 * quad + 4, :].bitcast(I32).rearrange("r (j c) -> j r c", j=4),
+            )
         nc.sync.dma_start(out=k_codes[1][:].bitcast(I32), in_=k_words[:, T // 2 : T])
         nc.sync.dma_start(idx2[:], offs2)
         nc.sync.dma_start(idx3[:], offs3)
@@ -113,13 +118,14 @@ def tile_attend_returnticket_two_kernel(
         for piece, width in enumerate(A_PIECES):
             cols = slice(lo, lo + width)
             k_half, k_lo = divmod(lo, T // 2)
+            plane, p_lo = divmod(lo, PLANE_COLS)
             bank = ps.tile([P, width], F32, name="a_bank%d" % piece)
             nc.tensor.matmul_mx(
                 out=bank[:],
                 lhsT=q_codes[:].bitcast(FP8X4),
                 lhsT_scale=q_plane[:],
                 rhs=k_codes[k_half][:, k_lo : k_lo + width].bitcast(FP8X4),
-                rhs_scale=k_plane[:, cols],
+                rhs_scale=k_plane[4 * plane : P, p_lo : p_lo + width],
                 start=True,
                 stop=True,
             )

@@ -22,7 +22,7 @@ PER_COL = 16
 HALF = SLOTS // 2
 A_PIECES = (256, 256, 256, 128, 128)
 B_PIECE = 512
-V_COLS = 704
+V_COLS = 672
 PLANE_COLS = T // 4
 V_QUERIES = 88
 
@@ -86,13 +86,13 @@ def tile_attend_returnticket_two_kernel(
         nc.sync.dma_start(out=q_raw[:], in_=query.rearrange("(p j) q -> p j q", j=PACK))
         k_words = keys_words[0].rearrange("p n t -> p (n t)").bitcast(I32)
         nc.sync.dma_start(out=k_codes[0][:].bitcast(I32), in_=k_words[:, 0 : T // 2])
-        nc.sync.dma_start(idx[:], offs)
         for quad in range(4):
             nc.sync.dma_start(
                 out=k_plane[32 * quad : 32 * quad + 16, :].bitcast(I32),
                 in_=keys_scales[0, 4 * quad : 4 * quad + 4, :].bitcast(I32).rearrange("r (j c) -> j r c", j=4),
             )
         nc.sync.dma_start(out=k_codes[1][:].bitcast(I32), in_=k_words[:, T // 2 : T])
+        nc.sync.dma_start(idx[:], offs)
         nc.sync.dma_start(idx2[:], offs2)
         nc.sync.dma_start(idx3[:], offs3)
         nc.sync.dma_start(out=n_codes[:].bitcast(I32), in_=notes_words[0].bitcast(I32))

from contextlib import ExitStack

import concourse.mybir as mybir

D, T, U, SLOTS, Q = 512, 1024, 1024, 512, 128
FLOPS = 2 * D * Q * (T + U)

F32 = mybir.dt.float32
BF16 = mybir.dt.bfloat16
I32 = mybir.dt.int32
U32 = mybir.dt.uint32
U16 = mybir.dt.uint16
U8 = mybir.dt.uint8
FP8X4 = mybir.dt.float8_e4m3fn_x4
FP4X4 = mybir.dt.float4_e2m1fn_x4
ALU = mybir.AluOpType
COPY = mybir.ActivationFunctionType.Copy

P = 128
PACK = 4
PER_COL = 16
HALF = SLOTS // 2
A_PIECES = (256, 256, 256, 128, 128)
B_PIECE = 512
V_COLS = 672
PLANE_COLS = T // 4
V_QUERIES = 88


def load_scale_rows(nc, plane, scales):
    for quad in range(4):
        nc.sync.dma_start(
            out=plane[32 * quad : 32 * quad + 4, :].bitcast(I32),
            in_=scales[0, 4 * quad : 4 * quad + 4, :].bitcast(I32),
        )


def half_of(offsets, h):
    cols = HALF // PER_COL
    return offsets[:, h * cols : (h + 1) * cols]


def gather_halves(nc, dst, window, offsets):
    nc.vector.tensor_copy(dst[:, 0:HALF], window[:].indirect(half_of(offsets, 0)))
    nc.scalar.activation(dst[:, HALF:SLOTS], window[:].indirect(half_of(offsets, 1)), COPY)


def tile_attend_returnticket_two_kernel(
    tc, query, keys_words, keys_scales, notes_words, notes_scales, offs, offs2, offs3, offs4, offs5, out
):
    nc = tc.nc
    with ExitStack() as ctx:
        sb = ctx.enter_context(tc.tile_pool(name="sb", bufs=1))
        ps = ctx.enter_context(tc.psum_pool(name="ps", bufs=1))

        idx = sb.tile([P, SLOTS // PER_COL], U16, name="idx")
        idx2 = sb.tile([P, SLOTS // PER_COL], U16, name="idx2")
        idx3 = sb.tile([P, SLOTS // PER_COL], U16, name="idx3")
        idx4 = sb.tile([P, SLOTS // PER_COL], U16, name="idx4")
        idx5 = sb.tile([P, SLOTS // PER_COL], U16, name="idx5")

        q_raw = sb.tile([P, PACK, Q], F32, name="q_raw")
        q_bf = sb.tile([P, Q, PACK], BF16, name="q_bf", align_bytes=64)
        q_codes = sb.tile([P, Q], U32, name="q_codes", align_bytes=64)
        q_plane = sb.tile([P, Q], U8, name="q_plane", align_bytes=64)
        k_codes = [sb.tile([P, T // 2], U32, name="k_codes%d" % h, align_bytes=64) for h in range(2)]
        k_plane = sb.tile([P, PLANE_COLS], U8, name="k_plane", align_bytes=64)
        n_codes = sb.tile([P, 2 * U], U8, name="n_codes", align_bytes=64)
        n_plane = sb.tile([P, U], U8, name="n_plane", align_bytes=64)

        a = sb.tile([P, T], F32, name="a")
        f1 = sb.tile([P, U], F32, name="f1")
        bb = sb.tile([P, U], F32, name="bb")
        f2 = sb.tile([P, T], F32, name="f2")
        aa = sb.tile([P, T], F32, name="aa")
        own = sb.tile([P, SLOTS], F32, name="own")
        back = sb.tile([P, SLOTS], F32, name="back")
        v = sb.tile([P, SLOTS], F32, name="v")
        res = sb.tile([P, SLOTS], F32, name="res")

        nc.vector.memset(k_plane[:].bitcast(U32), 0)
        nc.vector.memset(n_plane[:].bitcast(U32), 0)
        nc.vector.memset(f1[:], 0.0)
        nc.vector.memset(f2[:], 0.0)

        nc.sync.dma_start(out=q_raw[:], in_=query.rearrange("(p j) q -> p j q", j=PACK))
        k_words = keys_words[0].rearrange("p n t -> p (n t)").bitcast(I32)
        nc.sync.dma_start(out=k_codes[0][:].bitcast(I32), in_=k_words[:, 0 : T // 2])
        for quad in range(4):
            nc.sync.dma_start(
                out=k_plane[32 * quad : 32 * quad + 16, :].bitcast(I32),
                in_=keys_scales[0, 4 * quad : 4 * quad + 4, :].bitcast(I32).rearrange("r (j c) -> j r c", j=4),
            )
        nc.sync.dma_start(out=k_codes[1][:].bitcast(I32), in_=k_words[:, T // 2 : T])
        nc.sync.dma_start(idx[:], offs)
        nc.sync.dma_start(idx2[:], offs2)
        nc.sync.dma_start(idx3[:], offs3)
        nc.sync.dma_start(out=n_codes[:].bitcast(I32), in_=notes_words[0].bitcast(I32))
        load_scale_rows(nc, n_plane, notes_scales)
        nc.sync.dma_start(idx4[:], offs4)
        nc.sync.dma_start(idx5[:], offs5)

        nc.vector.tensor_copy(
            out=q_bf[:, 0:V_QUERIES, :].rearrange("p (c i) t -> p c t i", i=4),
            in_=q_raw[:, :, 0:V_QUERIES].rearrange("p t (c i) -> p c t i", i=4),
        )
        nc.scalar.activation(
            q_bf[:, V_QUERIES:Q, :].rearrange("p (c i) t -> p c t i", i=4),
            q_raw[:, :, V_QUERIES:Q].rearrange("p t (c i) -> p c t i", i=4),
            COPY,
        )
        nc.vector.quantize_mx(
            out=q_codes[:].bitcast(FP8X4), scales=q_plane[:], in_=q_bf[:].rearrange("p q t -> p (q t)")
        )

        a_banks = []
        lo = 0
        for piece, width in enumerate(A_PIECES):
            cols = slice(lo, lo + width)
            k_half, k_lo = divmod(lo, T // 2)
            plane, p_lo = divmod(lo, PLANE_COLS)
            bank = ps.tile([P, width], F32, name="a_bank%d" % piece)
            nc.tensor.matmul_mx(
                out=bank[:],
                lhsT=q_codes[:].bitcast(FP8X4),
                lhsT_scale=q_plane[:],
                rhs=k_codes[k_half][:, k_lo : k_lo + width].bitcast(FP8X4),
                rhs_scale=k_plane[4 * plane : P, p_lo : p_lo + width],
                start=True,
                stop=True,
            )
            if piece % 2 == 0:
                nc.scalar.activation(a[:, cols], bank[:], COPY)
            else:
                nc.vector.tensor_copy(a[:, cols], bank[:])
            a_banks.append((lo, width, bank))
            lo = lo + width

        b_banks = []
        for piece in range(U // B_PIECE):
            bank = ps.tile([P, B_PIECE], F32, name="b_bank%d" % piece)
            nc.tensor.matmul_mx(
                out=bank[:],
                lhsT=q_codes[:].bitcast(FP8X4),
                lhsT_scale=q_plane[:],
                rhs=n_codes[:, 2 * piece * B_PIECE : 2 * (piece + 1) * B_PIECE].bitcast(FP4X4),
                rhs_scale=n_plane[:, piece * B_PIECE : (piece + 1) * B_PIECE],
                start=True,
                stop=True,
            )
            b_banks.append(bank)

        gather_halves(nc, own, a, idx)
        b_tail = sb.tile([P, U - V_COLS], F32, name="b_tail")
        nc.scalar.activation(b_tail[:], b_banks[1][:, V_COLS - B_PIECE : B_PIECE], COPY)
        nc.vector.tensor_copy(f1[:].indirect(idx2[:]), own[:])
        nc.gpsimd.tensor_tensor(bb[:, V_COLS:U], f1[:, V_COLS:U], b_tail[:], ALU.subtract)
        for lo in range(0, V_COLS, B_PIECE):
            hi = min(lo + B_PIECE, V_COLS)
            nc.vector.tensor_tensor(bb[:, lo:hi], f1[:, lo:hi], b_banks[lo // B_PIECE][:, 0 : hi - lo], ALU.subtract)

        gather_halves(nc, back, bb, idx3)
        for h in range(2):
            cols = slice(h * HALF, (h + 1) * HALF)
            nc.vector.tensor_tensor(v[:, cols], back[:, cols], own[:, cols], ALU.max)
        nc.vector.tensor_copy(f2[:].indirect(idx4[:]), v[:])
        nc.gpsimd.tensor_tensor(aa[:, V_COLS:T], a[:, V_COLS:T], f2[:, V_COLS:T], ALU.subtract)
        for lo, width, bank in a_banks:
            hi = min(lo + width, V_COLS)
            if hi > lo:
                nc.vector.tensor_tensor(aa[:, lo:hi], bank[:, 0 : hi - lo], f2[:, lo:hi], ALU.subtract)

        gather_halves(nc, res, aa, idx5)
        nc.sync.dma_start(out=out[:, 0:HALF], in_=res[:, 0:HALF])
        nc.scalar.dma_start(out=out[:, HALF:SLOTS], in_=res[:, HALF:SLOTS])
